import numpy as np
CORES = [401,273,145,17]
N = 4
def setup_inputs(rng):
    return {"x": rng.standard_normal((N, 128, 128), dtype=np.float32)}
def reference(x):
    s = np.maximum.accumulate(x, axis=0)
    return {"y": s.astype(x.dtype)}

@@ -1,0 +1,57 @@
+from concourse.bass import DstId, RemoteDMATransfer
+
+SCRATCH = {
+    "a": ("sbuf", [128, 128], "float32"),
+    "b": ("sbuf", [128, 128], "float32"),
+}
+SEMAPHORES = ["loaded", "sent", "arrived", "stored"]
+
+MAX = 2
+OFF_CHIP = 0x00FF
+UPPER = 0xFF00
+ALL = 0xFFFF
+
+
+def rank_program(g, core, T, topo):
+    cores = T.cores
+    n = len(cores)
+    helper = [c - 1 for c in cores]
+    sem = T.sem
+
+    rank = T.rank_of(core)
+    if rank is not None:
+        g.sync.dma_start(T.b[:], T.x[:]).then_inc(sem.loaded, 16)
+        if rank == 0:
+            g.scalar.dma_start(T.y[:], T.x[:]).then_inc(sem.stored, 16)
+            dst, out, mask, k = helper[1], T.a, OFF_CHIP, 8
+        else:
+            dst, out, mask, k = helper[rank], T.b, ALL, 16
+        rid, pid = topo.addr(dst, core)
+        g.wait_ge(sem.loaded, 16)
+        g.remote_dma(out_ap=out[:], in_ap=T.b[:], remote_sem=sem.arrived, local_sem=sem.sent,
+                     pid=pid, routing_id=rid, dma_engine_mask=mask)
+        if rank > 0:
+            g.wait_ge(sem.arrived, 8 if rank < n - 1 else 16)
+            g.dma_start(T.y[:], T.a[:]).then_inc(sem.stored, 16)
+        g.wait_ge(sem.sent, k)
+        g.wait_ge(sem.stored, 16)
+        return
+
+    if core in helper[1:]:
+        r = helper.index(core)
+        g.wait_ge(sem.arrived, 8 + 16)
+        rid, pid = topo.addr(cores[r], core)
+        if r < n - 1:
+            rid2, pid2 = topo.addr(helper[r + 1], core)
+            g.remote_dma_fused([
+                RemoteDMATransfer(dst_ids=[DstId(rid=rid2, pnc=pid2)], dma_engine_mask=OFF_CHIP, remote_sem=sem.arrived,
+                                  srcs=[T.a[:], T.b[:]], dsts=[T.a[:]], alu_op=MAX),
+                RemoteDMATransfer(dst_ids=[DstId(rid=rid, pnc=pid)], dma_engine_mask=UPPER, remote_sem=sem.arrived,
+                                  srcs=[T.a[:], T.b[:]], dsts=[T.a[:]], alu_op=MAX),
+            ], local_sem=sem.sent)
+        else:
+            g.remote_dma_fused([
+                RemoteDMATransfer(dst_ids=[DstId(rid=rid, pnc=pid)], dma_engine_mask=ALL, remote_sem=sem.arrived,
+                                  srcs=[T.a[:], T.b[:]], dsts=[T.a[:]], alu_op=MAX),
+            ], local_sem=sem.sent)
+        g.wait_ge(sem.sent, 16)

@@ -1,57 +1,72 @@
 from concourse.bass import DstId, RemoteDMATransfer
 
+K = 2
+W = 128 * 128 // (128 * K)
+HELPER_CORES = (0, 4)
+
 SCRATCH = {
-    "a": ("sbuf", [128, 128], "float32"),
-    "b": ("sbuf", [128, 128], "float32"),
+    "own": ("dram", [K, 128, W], "float32"),
+    "res": ("dram", [K, 128, W], "float32"),
 }
 SEMAPHORES = ["loaded", "sent", "arrived", "stored"]
 
 MAX = 2
-OFF_CHIP = 0x00FF
-UPPER = 0xFF00
-ALL = 0xFFFF
+LOW8 = 0x00FF
+HIGH8 = 0xFF00
 
 
 def rank_program(g, core, T, topo):
     cores = T.cores
-    n = len(cores)
-    helper = [c - 1 for c in cores]
     sem = T.sem
+
+    def helpers_of(r):
+        base = cores[r] - cores[r] % 8
+        return [base + h for h in HELPER_CORES]
+
+    def dst_id(d):
+        rid, pid = topo.addr(d, core)
+        return DstId(rid=rid, pnc=pid)
 
     rank = T.rank_of(core)
     if rank is not None:
-        g.sync.dma_start(T.b[:], T.x[:]).then_inc(sem.loaded, 16)
+        g.sync.dma_start(T.own[:], T.x[:]).then_inc(sem.loaded, 16)
         if rank == 0:
             g.scalar.dma_start(T.y[:], T.x[:]).then_inc(sem.stored, 16)
-            dst, out, mask, k = helper[1], T.a, OFF_CHIP, 8
+        if rank == 0:
+            to, slot, engines = helpers_of(1), T.res[0], 8
+        elif rank == 3:
+            to, slot, engines = helpers_of(2), T.own[1], 8
         else:
-            dst, out, mask, k = helper[rank], T.b, ALL, 16
-        rid, pid = topo.addr(dst, core)
+            to, slot, engines = helpers_of(rank), T.own[0], 16
+        per = engines // K
         g.wait_ge(sem.loaded, 16)
-        g.remote_dma(out_ap=out[:], in_ap=T.b[:], remote_sem=sem.arrived, local_sem=sem.sent,
-                     pid=pid, routing_id=rid, dma_engine_mask=mask)
+        g.remote_dma_fused([
+            RemoteDMATransfer(dst_ids=[dst_id(to[k])], dma_engine_mask=((1 << per) - 1) << (per * k),
+                              remote_sem=sem.arrived, src=T.own[k], dst=slot)
+            for k in range(K)
+        ], local_sem=sem.sent)
         if rank > 0:
-            g.wait_ge(sem.arrived, 8 if rank < n - 1 else 16)
-            g.dma_start(T.y[:], T.a[:]).then_inc(sem.stored, 16)
-        g.wait_ge(sem.sent, k)
+            g.sync.wait_ge(sem.arrived, 8 * K)
+            g.sync.dma_start(T.y[:], T.res[:]).then_inc(sem.stored, 16)
+        g.wait_ge(sem.sent, engines)
         g.wait_ge(sem.stored, 16)
         return
 
-    if core in helper[1:]:
-        r = helper.index(core)
-        g.wait_ge(sem.arrived, 8 + 16)
-        rid, pid = topo.addr(cores[r], core)
-        if r < n - 1:
-            rid2, pid2 = topo.addr(helper[r + 1], core)
-            g.remote_dma_fused([
-                RemoteDMATransfer(dst_ids=[DstId(rid=rid2, pnc=pid2)], dma_engine_mask=OFF_CHIP, remote_sem=sem.arrived,
-                                  srcs=[T.a[:], T.b[:]], dsts=[T.a[:]], alu_op=MAX),
-                RemoteDMATransfer(dst_ids=[DstId(rid=rid, pnc=pid)], dma_engine_mask=UPPER, remote_sem=sem.arrived,
-                                  srcs=[T.a[:], T.b[:]], dsts=[T.a[:]], alu_op=MAX),
-            ], local_sem=sem.sent)
+    for r in (1, 2):
+        hs = helpers_of(r)
+        if core not in hs:
+            continue
+        k = hs.index(core)
+        pre, mine, x3 = T.res[0], T.own[0], T.own[1]
+        if r == 1:
+            g.wait_ge(sem.arrived, 4 + 8)
+            far = RemoteDMATransfer(dst_ids=[dst_id(helpers_of(2)[k])], dma_engine_mask=LOW8, remote_sem=sem.arrived,
+                                    srcs=[pre, mine], dsts=[T.res[0]], alu_op=MAX)
         else:
-            g.remote_dma_fused([
-                RemoteDMATransfer(dst_ids=[DstId(rid=rid, pnc=pid)], dma_engine_mask=ALL, remote_sem=sem.arrived,
-                                  srcs=[T.a[:], T.b[:]], dsts=[T.a[:]], alu_op=MAX),
-            ], local_sem=sem.sent)
+            g.wait_ge(sem.arrived, 8 + 8 + 4)
+            far = RemoteDMATransfer(dst_ids=[dst_id(cores[3])], dma_engine_mask=LOW8, remote_sem=sem.arrived,
+                                    srcs=[pre, mine, x3], dsts=[T.res[k]], alu_op=MAX)
+        near = RemoteDMATransfer(dst_ids=[dst_id(cores[r])], dma_engine_mask=HIGH8, remote_sem=sem.arrived,
+                                 srcs=[pre, mine], dsts=[T.res[k]], alu_op=MAX)
+        g.remote_dma_fused([far, near], local_sem=sem.sent)
         g.wait_ge(sem.sent, 16)

@@ -1,7 +1,7 @@
 from concourse.bass import DstId, RemoteDMATransfer
 
 K = 2
-W = 128 * 128 // (128 * K)
+W = 128 // K
 HELPER_CORES = (0, 4)
 
 SCRATCH = {

from concourse.bass import DstId, RemoteDMATransfer

K = 2
W = 128 // K
HELPER_CORES = (0, 4)

SCRATCH = {
    "own": ("dram", [K, 128, W], "float32"),
    "res": ("dram", [K, 128, W], "float32"),
}
SEMAPHORES = ["loaded", "sent", "arrived", "stored"]

MAX = 2
LOW8 = 0x00FF
HIGH8 = 0xFF00


def rank_program(g, core, T, topo):
    cores = T.cores
    sem = T.sem

    def helpers_of(r):
        base = cores[r] - cores[r] % 8
        return [base + h for h in HELPER_CORES]

    def dst_id(d):
        rid, pid = topo.addr(d, core)
        return DstId(rid=rid, pnc=pid)

    rank = T.rank_of(core)
    if rank is not None:
        g.sync.dma_start(T.own[:], T.x[:]).then_inc(sem.loaded, 16)
        if rank == 0:
            g.scalar.dma_start(T.y[:], T.x[:]).then_inc(sem.stored, 16)
        if rank == 0:
            to, slot, engines = helpers_of(1), T.res[0], 8
        elif rank == 3:
            to, slot, engines = helpers_of(2), T.own[1], 8
        else:
            to, slot, engines = helpers_of(rank), T.own[0], 16
        per = engines // K
        g.wait_ge(sem.loaded, 16)
        g.remote_dma_fused([
            RemoteDMATransfer(dst_ids=[dst_id(to[k])], dma_engine_mask=((1 << per) - 1) << (per * k),
                              remote_sem=sem.arrived, src=T.own[k], dst=slot)
            for k in range(K)
        ], local_sem=sem.sent)
        if rank > 0:
            g.sync.wait_ge(sem.arrived, 8 * K)
            g.sync.dma_start(T.y[:], T.res[:]).then_inc(sem.stored, 16)
        g.wait_ge(sem.sent, engines)
        g.wait_ge(sem.stored, 16)
        return

    for r in (1, 2):
        hs = helpers_of(r)
        if core not in hs:
            continue
        k = hs.index(core)
        pre, mine, x3 = T.res[0], T.own[0], T.own[1]
        if r == 1:
            g.wait_ge(sem.arrived, 4 + 8)
            far = RemoteDMATransfer(dst_ids=[dst_id(helpers_of(2)[k])], dma_engine_mask=LOW8, remote_sem=sem.arrived,
                                    srcs=[pre, mine], dsts=[T.res[0]], alu_op=MAX)
        else:
            g.wait_ge(sem.arrived, 8 + 8 + 4)
            far = RemoteDMATransfer(dst_ids=[dst_id(cores[3])], dma_engine_mask=LOW8, remote_sem=sem.arrived,
                                    srcs=[pre, mine, x3], dsts=[T.res[k]], alu_op=MAX)
        near = RemoteDMATransfer(dst_ids=[dst_id(cores[r])], dma_engine_mask=HIGH8, remote_sem=sem.arrived,
                                 srcs=[pre, mine], dsts=[T.res[k]], alu_op=MAX)
        g.remote_dma_fused([far, near], local_sem=sem.sent)
        g.wait_ge(sem.sent, 16)
